import numpy as np
import ml_dtypes


def mxq(x, axis, fmt="e4m3"):
    dtype, down = {"e4m3": (ml_dtypes.float8_e4m3fn, 7), "e5m2": (ml_dtypes.float8_e5m2, 14)}[fmt]
    v = np.moveaxis(np.asarray(x, np.float32).astype(ml_dtypes.bfloat16).astype(np.float64), axis, -1)
    blocks = v.reshape(v.shape[:-1] + (-1, 32))
    amax = np.abs(blocks).max(-1, keepdims=True)
    byte = np.maximum(np.where(amax > 0, np.frexp(amax)[1] - 1 + 127, 0) - down, 1)
    scale = np.exp2(byte - 127.0)
    codes = (blocks / scale).astype(np.float32).astype(dtype).astype(np.float64)
    return np.moveaxis((codes * scale).reshape(v.shape), -1, axis)


WIDE = False


def mx_kscale(k):
    if not WIDE:
        return np.ones(k)
    levels = np.array([10, -10, 5, -5, 0])
    if k % 512:
        return np.exp2(np.random.permutation(np.resize(levels, k // 32))).repeat(32)
    a = np.empty((k // 512, 16))
    for p in range(k // 512):
        a[p, :8] = np.random.permutation(np.resize(levels, 8))
        for g in range(8):
            far = levels[np.abs(levels - a[p, g]) >= 10]
            a[p, g + 8] = far[np.random.randint(len(far))]
    return np.exp2(a.ravel()).repeat(32)


def f64(x):
    return np.asarray(x).astype(np.float64)


def striped(idx):
    return np.tile(idx.reshape(-1, 16).T, (8, 1)).astype(np.uint16)


def unstriped(offs):
    return offs[:16].T.reshape(-1).astype(np.int64)


def striped8(idx):
    return np.concatenate([x.reshape(-1, 16).T for x in idx]).astype(np.uint16)


def runs(offs, k):
    lists = np.stack([offs[16 * r : 16 * r + 16].T.reshape(-1) for r in range(8)]).astype(np.int64)
    return lists[np.arange(k) % 512 // 64]


def pack_weight(w):
    k, n = w.shape
    w = f64(np.asarray(w, np.float32).astype(ml_dtypes.bfloat16)).reshape(k // 32, 32, n)
    amax = np.abs(w).max(1)
    byte = np.clip(np.where(amax > 0, np.frexp(amax)[1] - 1 + 127 - 7, 1), 1, 254)
    scaled = (w * np.exp2(127.0 - byte)[:, None, :]).reshape(k, n).astype(np.float32)
    words = np.ascontiguousarray(scaled.reshape(k // 512, 128, 4, n).transpose(0, 1, 3, 2)).astype(ml_dtypes.float8_e4m3fn).view(np.uint8)
    return words, np.ascontiguousarray(byte.astype(np.uint8).reshape(k // 512, 16, n))


def unpack_weight(words, scales):
    g, p, n, _ = words.shape
    vals = np.ascontiguousarray(words).view(ml_dtypes.float8_e4m3fn).astype(np.float64) * np.repeat(np.exp2(scales.astype(np.float64) - 127.0), 8, axis=1)[..., None]
    return vals.transpose(0, 1, 3, 2).reshape(g * 512, n)


def relu(v):
    return np.maximum(v, 0.0)


K, T, S, N, H, U = 512, 2048, 256, 512, 512, 1024


def setup_inputs():
    n = np.random.standard_normal
    s = mx_kscale(K)[:, None]
    u = mx_kscale(H)
    packed_xT = pack_weight(n((K, T)) * s)
    packed_w1 = pack_weight(n((K, H)) / np.sqrt(2 * K) / s)
    packed_w2 = pack_weight(n((K, H)) / np.sqrt(2 * K) / s)
    packed_w3 = pack_weight(n((H, N)) / np.sqrt(H) / u[:, None])
    return {
        "x_words": packed_xT[0],
        "x_scales": packed_xT[1],
        "w1_words": packed_w1[0],
        "w1_scales": packed_w1[1],
        "w2_words": packed_w2[0],
        "w2_scales": packed_w2[1],
        "gn": (np.random.uniform(0.5, 1.5, (H, 1)) * u[:, None]).astype(np.float32),
        "w3_words": packed_w3[0],
        "w3_scales": packed_w3[1],
        "offs": striped8(np.random.randint(0, T, (8, S))),
        "hz": striped8(np.random.randint(0, T, (8, S))),
        "n1": striped(np.random.permutation(S)),
        "n2": striped(np.random.permutation(S)),
        "n3": striped(np.random.permutation(U)[:S]),
        "n4": striped(np.random.permutation(S)),
    }


def reference(x_words, x_scales, w1_words, w1_scales, w2_words, w2_scales, gn, w3_words, w3_scales, offs, hz, n1, n2, n3, n4):
    xq = unpack_weight(x_words, x_scales)[np.arange(K)[:, None], runs(offs, K)]
    x_hz = unpack_weight(x_words, x_scales)[np.arange(K)[:, None], runs(hz, K)]
    y = unpack_weight(w1_words, w1_scales).T @ xq + unpack_weight(w2_words, w2_scales).T @ x_hz
    ds = np.zeros((H, S))
    ds[:, unstriped(n1)] = y
    z = f64(gn) * (np.maximum(y, ds[:, unstriped(n2)]))
    h = unpack_weight(w3_words, w3_scales).T @ mxq(z, 0, "e4m3")
    nw = h - (relu(h[:, unstriped(n4)]))
    out = np.zeros((N, U))
    out[:, unstriped(n3)] = nw
    return out

@@ -1,0 +1,201 @@
+from contextlib import ExitStack
+
+import concourse.mybir as mybir
+
+K, T, S, N, H, U = 512, 2048, 256, 512, 512, 1024
+FLOPS = 2 * S * (2 * K * H + H * N)
+
+F32 = mybir.dt.float32
+BF16 = mybir.dt.bfloat16
+I32 = mybir.dt.int32
+U32 = mybir.dt.uint32
+U16 = mybir.dt.uint16
+U8 = mybir.dt.uint8
+FP8X4 = mybir.dt.float8_e4m3fn_x4
+ALU = mybir.AluOpType
+COPY = mybir.ActivationFunctionType.Copy
+
+P = 128
+PACK = 4
+HALF = S // 2
+WIN = 2 * S
+
+
+def words_view(words):
+    return words[0].rearrange("p n t -> p (n t)").bitcast(I32)
+
+
+def tile_picked_dhlrelaypagez_none_p_kernel(tc, x_words, x_scales, w1_words, w1_scales, w2_words, w2_scales, gn, w3_words, w3_scales, offs, hz, n1, n2, n3, n4, out):
+    nc = tc.nc
+    with ExitStack() as ctx:
+        lists = ctx.enter_context(tc.tile_pool(name="lists", bufs=1))
+        keep = ctx.enter_context(tc.tile_pool(name="keep", bufs=1))
+        shared = ctx.enter_context(tc.tile_pool(name="shared", bufs=1))
+        psum = ctx.enter_context(tc.psum_pool(name="psum", bufs=1))
+
+        def load_list(name, src):
+            tile = lists.tile([P, S // 16], U16, name=name)
+            nc.sync.dma_start(tile[:], src)
+            return tile
+
+        offs_t = load_list("offs_t", offs)
+        hz_t = load_list("hz_t", hz)
+
+        x_bytes = shared.tile([P, T], U8, name="x_bytes", offset=12288)
+        nc.vector.memset(x_bytes[:].bitcast(I32), 0)
+        nc.sync.dma_start(x_bytes[0:P:8, :].bitcast(I32), x_scales[0].bitcast(I32))
+
+        def load_plane(plane, scales, clearer, queue):
+            clearer.memset(plane[:].bitcast(I32), 0)
+            for q in range(4):
+                queue.dma_start(plane[32 * q : 32 * q + 4, :].bitcast(I32), scales[0].bitcast(I32)[4 * q : 4 * q + 4, :])
+
+        w_rows = [keep.tile([P, H], U8, name="w_rows%d" % w) for w in range(2)]
+        load_plane(w_rows[0], w1_scales, nc.vector, nc.scalar)
+        load_plane(w_rows[1], w2_scales, nc.gpsimd, nc.gpsimd)
+
+        x_win = shared.tile([P, T], U32, name="x_win", offset=0)
+        nc.sync.dma_start(x_win[:].bitcast(I32), words_view(x_words))
+        w_raw = []
+        for w, words in enumerate((w1_words, w2_words)):
+            raw = shared.tile([P, H], U32, name="w_raw%d" % w, offset=8192 + 2048 * w)
+            nc.sync.dma_start(raw[:].bitcast(I32), words_view(words))
+            w_raw.append(raw)
+
+        x_plane = keep.tile([P, 2 * S], U8, name="x_plane", align_bytes=64)
+        nc.vector.memset(x_plane[:].bitcast(I32), 0)
+        zero = keep.tile([P, 1], F32, name="zero")
+        nc.vector.memset(zero[:], 0.0)
+        pages = [keep.tile([P, U], F32, name="page0")]
+        nc.scalar.activation(pages[0][:], zero[:].to_broadcast([P, U]), COPY)
+
+        got_bytes = keep.tile([P, 2 * S], U8, name="got_bytes", tag="bytes", align_bytes=64)
+        nc.vector.tensor_copy(got_bytes[:, 0:S], x_bytes[:].indirect(offs_t[:]))
+        nc.vector.tensor_copy(got_bytes[:, S : 2 * S], x_bytes[:].indirect(hz_t[:]))
+        for q in range(4):
+            queue = nc.sync if q == 2 else nc.scalar
+            queue.dma_start(x_plane[32 * q : 32 * q + 4, :].bitcast(I32), got_bytes[32 * q : 32 * q + 32 : 8, :].bitcast(I32))
+
+        w_plane = [keep.tile([P, PACK, P], U8, name="w_plane%d" % w, align_bytes=64) for w in range(2)]
+        dealt_rows = [rows[:].rearrange("p (m t) -> p t m", t=PACK) for rows in w_rows]
+        nc.vector.tensor_copy(w_plane[0][:], dealt_rows[0])
+
+        got_words = []
+        for w, picks in enumerate((offs_t, hz_t)):
+            got = keep.tile([P, S], U32, name="got_words%d" % w, align_bytes=64)
+            nc.vector.tensor_copy(got[:], x_win[:].indirect(picks[:]))
+            got_words.append(got)
+        nc.vector.tensor_copy(w_plane[1][:, 0, :], dealt_rows[1][:, 0, :])
+        nc.vector.tensor_copy(w_plane[1][:, 1:PACK, :], dealt_rows[1][:, 1:PACK, :])
+
+        w_dealt = [keep.tile([P, PACK, P], U32, name="w_dealt%d" % w, align_bytes=64) for w in range(2)]
+        raw_words = [raw[:].rearrange("p (m t) -> p m t", t=PACK) for raw in w_raw]
+        nc.scalar.copy(w_dealt[0][:].rearrange("p t m -> p m t"), raw_words[0])
+        nc.scalar.copy(w_dealt[1][:, 0, :], raw_words[1][:, :, 0])
+        nc.scalar.copy(w_dealt[1][:, 1:PACK, :].rearrange("p t m -> p m t"), raw_words[1][:, :, 1:PACK])
+
+        n1_t = load_list("n1_t", n1)
+        n2_t = load_list("n2_t", n2)
+        gain = keep.tile([P, PACK], F32, name="gain")
+        nc.sync.dma_start(gain[:], gn.rearrange("(p t) o -> p (t o)", t=PACK))
+        n4_t = load_list("n4_t", n4)
+        n3_t = load_list("n3_t", n3)
+        w3 = shared.tile([P, N], U32, name="w3", offset=12288, align_bytes=64)
+        nc.sync.dma_start(w3[:].bitcast(I32), words_view(w3_words))
+
+        w3_plane = keep.tile([P, N], U8, name="w3_plane", tag="bytes", align_bytes=64)
+        load_plane(w3_plane, w3_scales, nc.gpsimd, nc.sync)
+
+        y = []
+        for t in range(PACK):
+            acc = psum.tile([P, S], F32, name="y_acc%d" % t, tag="bank%d" % t)
+            for w in range(2):
+                nc.tensor.matmul_mx(
+                    out=acc[:],
+                    lhsT=w_dealt[w][:, t, :].bitcast(FP8X4),
+                    lhsT_scale=w_plane[w][:, t, :],
+                    rhs=got_words[w][:].bitcast(FP8X4),
+                    rhs_scale=x_plane[:, w * S : (w + 1) * S],
+                    start=(w == 0),
+                    stop=(w == 1),
+                )
+            y_t = keep.tile([P, S], F32, name="y%d" % t)
+            nc.vector.tensor_copy(y_t[:], acc[:])
+            y.append(y_t)
+
+        for m in range(1, N // P):
+            page = shared.tile([P, U], F32, name="page%d" % m, offset=4096 * (m - 1))
+            nc.vector.memset(page[:], 0.0)
+            pages.append(page)
+
+        z = [keep.tile([P, HALF, PACK], BF16, name="z%d" % h, align_bytes=64) for h in range(2)]
+        ds = [keep.tile([P, WIN], F32, name="ds%d" % t) for t in range(PACK)]
+
+        def send(t):
+            nc.scalar.activation(ds[t][:].indirect(n1_t[:]), y[t][:], COPY)
+
+        def compare(t, pieces):
+            fetched = keep.tile([P, S], F32, name="ds_got%d" % t)
+            larger = keep.tile([P, S], F32, name="larger%d" % t)
+            for lo, hi in pieces:
+                nc.scalar.activation(fetched[:, lo:hi], ds[t][:].indirect(n2_t[:, lo // 16 : hi // 16]), COPY)
+            for lo, hi in pieces:
+                nc.vector.tensor_tensor(larger[:, lo:hi], fetched[:, lo:hi], y[t][:, lo:hi], ALU.max)
+            for h in range(2):
+                nc.vector.tensor_scalar(z[h][:, :, t], larger[:, h * HALF : (h + 1) * HALF], gain[:, t : t + 1], None, ALU.mult)
+
+        send(0)
+        send(1)
+        compare(0, [(0, S)])
+        send(2)
+        compare(1, [(0, S)])
+        compare(2, [(0, S)])
+        send(3)
+        compare(3, [(0, HALF), (HALF, S)])
+
+        z_words, z_plane = [], []
+        for h in range(2):
+            words = keep.tile([P, HALF], U32, name="z_words%d" % h, align_bytes=64)
+            plane = keep.tile([P, HALF], U8, name="z_plane%d" % h, align_bytes=64)
+            nc.vector.quantize_mx(out=words[:].bitcast(FP8X4), scales=plane[:], in_=z[h][:].rearrange("p j t -> p (j t)"))
+            z_words.append(words)
+            z_plane.append(plane)
+
+        h_acc = {}
+        for h in range(2):
+            for m in range(N // P):
+                acc = psum.tile([P, HALF], F32, name="h_acc%d_%d" % (m, h), tag="bank%d" % (m + 4 * (1 - h)))
+                nc.tensor.matmul_mx(
+                    out=acc[:],
+                    lhsT=w3[:, m * P : (m + 1) * P].bitcast(FP8X4),
+                    lhsT_scale=w3_plane[:, m * P : (m + 1) * P],
+                    rhs=z_words[h][:].bitcast(FP8X4),
+                    rhs_scale=z_plane[h][:],
+                    start=True,
+                    stop=True,
+                )
+                h_acc[m, h] = acc
+
+        nw = []
+
+        def fetch(m):
+            positive = keep.tile([P, WIN], F32, name="positive%d" % m)
+            for h in range(2):
+                nc.vector.tensor_scalar(positive[:, h * HALF : (h + 1) * HALF], h_acc[m, h][:], 0.0, None, ALU.max)
+            fetched = keep.tile([P, S], F32, name="h_got%d" % m)
+            nc.scalar.activation(fetched[:], positive[:].indirect(n4_t[:]), COPY)
+            nw_m = keep.tile([P, S], F32, name="nw%d" % m)
+            for h in range(2):
+                cols = slice(h * HALF, (h + 1) * HALF)
+                nc.vector.tensor_tensor(nw_m[:, cols], h_acc[m, h][:], fetched[:, cols], ALU.subtract)
+            nw.append(nw_m)
+
+        def place(m):
+            nc.scalar.activation(pages[m][:].indirect(n3_t[:]), nw[m][:], COPY)
+            nc.sync.dma_start(out[m * P : (m + 1) * P, :], pages[m][:])
+
+        fetch(0)
+        for m in range(1, N // P):
+            fetch(m)
+            place(m - 1)
+        place(N // P - 1)

@@ -41,70 +41,68 @@ def tile_picked_dhlrelaypagez_none_p_kernel(tc, x_words, x_scales, w1_words, w1_
         offs_t = load_list("offs_t", offs)
         hz_t = load_list("hz_t", hz)
 
-        x_bytes = shared.tile([P, T], U8, name="x_bytes", offset=12288)
+        x_bytes = keep.tile([P, T], U8, name="x_bytes")
         nc.vector.memset(x_bytes[:].bitcast(I32), 0)
-        nc.sync.dma_start(x_bytes[0:P:8, :].bitcast(I32), x_scales[0].bitcast(I32))
+        w_rows = keep.tile([P, 2 * H], U8, name="w_rows", tag="rows", align_bytes=64)
+        nc.gpsimd.memset(w_rows[:].bitcast(I32), 0)
+        for w, scales in enumerate((w1_scales, w2_scales)):
+            nc.scalar.dma_start(w_rows[0:16, w * H : (w + 1) * H].bitcast(I32), scales[0].bitcast(I32))
+        nc.scalar.dma_start(x_bytes[0:P:8, :].bitcast(I32), x_scales[0].bitcast(I32))
 
-        def load_plane(plane, scales, clearer, queue):
-            clearer.memset(plane[:].bitcast(I32), 0)
-            for q in range(4):
-                queue.dma_start(plane[32 * q : 32 * q + 4, :].bitcast(I32), scales[0].bitcast(I32)[4 * q : 4 * q + 4, :])
-
-        w_rows = [keep.tile([P, H], U8, name="w_rows%d" % w) for w in range(2)]
-        load_plane(w_rows[0], w1_scales, nc.vector, nc.scalar)
-        load_plane(w_rows[1], w2_scales, nc.gpsimd, nc.gpsimd)
-
-        x_win = shared.tile([P, T], U32, name="x_win", offset=0)
-        nc.sync.dma_start(x_win[:].bitcast(I32), words_view(x_words))
-        w_raw = []
-        for w, words in enumerate((w1_words, w2_words)):
-            raw = shared.tile([P, H], U32, name="w_raw%d" % w, offset=8192 + 2048 * w)
-            nc.sync.dma_start(raw[:].bitcast(I32), words_view(words))
-            w_raw.append(raw)
-
-        x_plane = keep.tile([P, 2 * S], U8, name="x_plane", align_bytes=64)
-        nc.vector.memset(x_plane[:].bitcast(I32), 0)
         zero = keep.tile([P, 1], F32, name="zero")
         nc.vector.memset(zero[:], 0.0)
         pages = [keep.tile([P, U], F32, name="page0")]
         nc.scalar.activation(pages[0][:], zero[:].to_broadcast([P, U]), COPY)
 
-        got_bytes = keep.tile([P, 2 * S], U8, name="got_bytes", tag="bytes", align_bytes=64)
+        gain = keep.tile([P, PACK], F32, name="gain")
+        nc.gpsimd.dma_start(gain[:], gn.rearrange("(p t) o -> p (t o)", t=PACK))
+        x_plane = keep.tile([P, 2 * S], U8, name="x_plane", align_bytes=64)
+        nc.vector.memset(x_plane[:].bitcast(I32), 0)
+
+        w_raw = [keep.tile([P, H], U32, name="w_raw%d" % w) for w in range(2)]
+        nc.sync.dma_start(w_raw[0][:].bitcast(I32), words_view(w1_words))
+        n1_t = load_list("n1_t", n1)
+        x_win = shared.tile([P, T], U32, name="x_win", offset=0)
+        nc.sync.dma_start(x_win[:].bitcast(I32), words_view(x_words))
+        for q in range(1, 4):
+            nc.sync.dma_start(w_rows[32 * q : 32 * q + 4, :].bitcast(I32), w_rows[4 * q : 4 * q + 4, :].bitcast(I32))
+        nc.sync.dma_start(w_raw[1][:].bitcast(I32), words_view(w2_words))
+
+        got_bytes = shared.tile([P, 2 * S], U8, name="got_bytes", offset=12288, align_bytes=64)
         nc.vector.tensor_copy(got_bytes[:, 0:S], x_bytes[:].indirect(offs_t[:]))
         nc.vector.tensor_copy(got_bytes[:, S : 2 * S], x_bytes[:].indirect(hz_t[:]))
         for q in range(4):
-            queue = nc.sync if q == 2 else nc.scalar
-            queue.dma_start(x_plane[32 * q : 32 * q + 4, :].bitcast(I32), got_bytes[32 * q : 32 * q + 32 : 8, :].bitcast(I32))
+            nc.sync.dma_start(x_plane[32 * q : 32 * q + 4, :].bitcast(I32), got_bytes[32 * q : 32 * q + 32 : 8, :].bitcast(I32))
 
-        w_plane = [keep.tile([P, PACK, P], U8, name="w_plane%d" % w, align_bytes=64) for w in range(2)]
-        dealt_rows = [rows[:].rearrange("p (m t) -> p t m", t=PACK) for rows in w_rows]
-        nc.vector.tensor_copy(w_plane[0][:], dealt_rows[0])
 
         got_words = []
         for w, picks in enumerate((offs_t, hz_t)):
-            got = keep.tile([P, S], U32, name="got_words%d" % w, align_bytes=64)
+            got = shared.tile([P, S], U32, name="got_words%d" % w, offset=24576 + 1024 * w, align_bytes=64)
             nc.vector.tensor_copy(got[:], x_win[:].indirect(picks[:]))
             got_words.append(got)
-        nc.vector.tensor_copy(w_plane[1][:, 0, :], dealt_rows[1][:, 0, :])
-        nc.vector.tensor_copy(w_plane[1][:, 1:PACK, :], dealt_rows[1][:, 1:PACK, :])
+        w_plane = [shared.tile([P, 2, P], U8, name="w_plane%d" % t, offset=256 * t, align_bytes=64) for t in range(PACK)]
+        rows_by_tile = w_rows[:].rearrange("p (w m t) -> p w m t", w=2, t=PACK)
+        for w in range(2):
+            nc.vector.tensor_copy(w_plane[0][:, w, :], rows_by_tile[:, w, :, 0])
+        for t in range(1, PACK):
+            nc.vector.tensor_copy(w_plane[t][:], rows_by_tile[:, :, :, t])
 
-        w_dealt = [keep.tile([P, PACK, P], U32, name="w_dealt%d" % w, align_bytes=64) for w in range(2)]
+        w_dealt = [shared.tile([P, PACK, P], U32, name="w_dealt%d" % w, offset=16384 + 4096 * w, align_bytes=64) for w in range(2)]
         raw_words = [raw[:].rearrange("p (m t) -> p m t", t=PACK) for raw in w_raw]
         nc.scalar.copy(w_dealt[0][:].rearrange("p t m -> p m t"), raw_words[0])
         nc.scalar.copy(w_dealt[1][:, 0, :], raw_words[1][:, :, 0])
         nc.scalar.copy(w_dealt[1][:, 1:PACK, :].rearrange("p t m -> p m t"), raw_words[1][:, :, 1:PACK])
 
-        n1_t = load_list("n1_t", n1)
         n2_t = load_list("n2_t", n2)
-        gain = keep.tile([P, PACK], F32, name="gain")
-        nc.sync.dma_start(gain[:], gn.rearrange("(p t) o -> p (t o)", t=PACK))
         n4_t = load_list("n4_t", n4)
         n3_t = load_list("n3_t", n3)
         w3 = shared.tile([P, N], U32, name="w3", offset=12288, align_bytes=64)
         nc.sync.dma_start(w3[:].bitcast(I32), words_view(w3_words))
 
-        w3_plane = keep.tile([P, N], U8, name="w3_plane", tag="bytes", align_bytes=64)
-        load_plane(w3_plane, w3_scales, nc.gpsimd, nc.sync)
+        w3_plane = keep.tile([P, N], U8, name="w3_plane", tag="rows", align_bytes=64)
+        nc.vector.memset(w3_plane[:].bitcast(I32), 0)
+        for q in range(4):
+            nc.sync.dma_start(w3_plane[32 * q : 32 * q + 4, :].bitcast(I32), w3_scales[0].bitcast(I32)[4 * q : 4 * q + 4, :])
 
         y = []
         for t in range(PACK):
@@ -113,7 +111,7 @@ def tile_picked_dhlrelaypagez_none_p_kernel(tc, x_words, x_scales, w1_words, w1_
                 nc.tensor.matmul_mx(
                     out=acc[:],
                     lhsT=w_dealt[w][:, t, :].bitcast(FP8X4),
-                    lhsT_scale=w_plane[w][:, t, :],
+                    lhsT_scale=w_plane[t][:, w, :],
                     rhs=got_words[w][:].bitcast(FP8X4),
                     rhs_scale=x_plane[:, w * S : (w + 1) * S],
                     start=(w == 0),
@@ -124,10 +122,11 @@ def tile_picked_dhlrelaypagez_none_p_kernel(tc, x_words, x_scales, w1_words, w1_
             y.append(y_t)
 
         for m in range(1, N // P):
-            page = shared.tile([P, U], F32, name="page%d" % m, offset=4096 * (m - 1))
+            page = shared.tile([P, U], F32, name="page%d" % m, offset=16384 + 4096 * (m - 1))
             nc.vector.memset(page[:], 0.0)
             pages.append(page)
 
+        halves = [(0, HALF), (HALF, S)]
         z = [keep.tile([P, HALF, PACK], BF16, name="z%d" % h, align_bytes=64) for h in range(2)]
         ds = [keep.tile([P, WIN], F32, name="ds%d" % t) for t in range(PACK)]
 
@@ -151,43 +150,41 @@ def tile_picked_dhlrelaypagez_none_p_kernel(tc, x_words, x_scales, w1_words, w1_
         compare(1, [(0, S)])
         compare(2, [(0, S)])
         send(3)
-        compare(3, [(0, HALF), (HALF, S)])
+        compare(3, halves)
 
-        z_words, z_plane = [], []
-        for h in range(2):
-            words = keep.tile([P, HALF], U32, name="z_words%d" % h, align_bytes=64)
-            plane = keep.tile([P, HALF], U8, name="z_plane%d" % h, align_bytes=64)
-            nc.vector.quantize_mx(out=words[:].bitcast(FP8X4), scales=plane[:], in_=z[h][:].rearrange("p j t -> p (j t)"))
-            z_words.append(words)
-            z_plane.append(plane)
+        z_words = keep.tile([P, S], U32, name="z_words", align_bytes=64)
+        z_plane = keep.tile([P, S], U8, name="z_plane", align_bytes=64)
+        for h, (lo, hi) in enumerate(halves):
+            nc.vector.quantize_mx(out=z_words[:, lo:hi].bitcast(FP8X4), scales=z_plane[:, lo:hi], in_=z[h][:].rearrange("p j t -> p (j t)"))
 
-        h_acc = {}
-        for h in range(2):
-            for m in range(N // P):
-                acc = psum.tile([P, HALF], F32, name="h_acc%d_%d" % (m, h), tag="bank%d" % (m + 4 * (1 - h)))
+        h_acc = []
+        for m in range(N // P):
+            accs = []
+            for lo, hi in halves if m == 0 else [(0, S)]:
+                acc = psum.tile([P, hi - lo], F32, name="h_acc%d_%d" % (m, lo), tag="bank%d" % (m + 4 - 4 * (lo // HALF)))
                 nc.tensor.matmul_mx(
                     out=acc[:],
                     lhsT=w3[:, m * P : (m + 1) * P].bitcast(FP8X4),
                     lhsT_scale=w3_plane[:, m * P : (m + 1) * P],
-                    rhs=z_words[h][:].bitcast(FP8X4),
-                    rhs_scale=z_plane[h][:],
+                    rhs=z_words[:, lo:hi].bitcast(FP8X4),
+                    rhs_scale=z_plane[:, lo:hi],
                     start=True,
                     stop=True,
                 )
-                h_acc[m, h] = acc
+                accs.append((acc, slice(lo, hi)))
+            h_acc.append(accs)
 
         nw = []
 
         def fetch(m):
             positive = keep.tile([P, WIN], F32, name="positive%d" % m)
-            for h in range(2):
-                nc.vector.tensor_scalar(positive[:, h * HALF : (h + 1) * HALF], h_acc[m, h][:], 0.0, None, ALU.max)
+            for acc, cols in h_acc[m]:
+                nc.vector.tensor_scalar(positive[:, cols], acc[:], 0.0, None, ALU.max)
             fetched = keep.tile([P, S], F32, name="h_got%d" % m)
             nc.scalar.activation(fetched[:], positive[:].indirect(n4_t[:]), COPY)
             nw_m = keep.tile([P, S], F32, name="nw%d" % m)
-            for h in range(2):
-                cols = slice(h * HALF, (h + 1) * HALF)
-                nc.vector.tensor_tensor(nw_m[:, cols], h_acc[m, h][:], fetched[:, cols], ALU.subtract)
+            for acc, cols in h_acc[m]:
+                nc.vector.tensor_tensor(nw_m[:, cols], acc[:], fetched[:, cols], ALU.subtract)
             nw.append(nw_m)
 
         def place(m):

@@ -17,8 +17,17 @@ COPY = mybir.ActivationFunctionType.Copy
 
 P = 128
 PACK = 4
+QUADS = 4
+GROUP = 16
 HALF = S // 2
+WHOLE = [(0, S)]
+HALVES = [(0, HALF), (HALF, S)]
 WIN = 2 * S
+
+AT_X_WORDS = 0
+AT_GOT_BYTES = 12288
+AT_PAGES = 16384
+PAGE_BYTES = 4 * U
 
 
 def words_view(words):
@@ -34,20 +43,22 @@ def tile_picked_dhlrelaypagez_none_p_kernel(tc, x_words, x_scales, w1_words, w1_
         psum = ctx.enter_context(tc.psum_pool(name="psum", bufs=1))
 
         def load_list(name, src):
-            tile = lists.tile([P, S // 16], U16, name=name)
+            tile = lists.tile([P, S // GROUP], U16, name=name)
             nc.sync.dma_start(tile[:], src)
             return tile
+
+        def quad_rows(plane, q):
+            return plane[32 * q : 32 * q + 4, :].bitcast(I32)
 
         offs_t = load_list("offs_t", offs)
         hz_t = load_list("hz_t", hz)
 
-        x_bytes = keep.tile([P, T], U8, name="x_bytes")
-        nc.vector.memset(x_bytes[:].bitcast(I32), 0)
         w_rows = keep.tile([P, 2 * H], U8, name="w_rows", tag="rows", align_bytes=64)
-        nc.gpsimd.memset(w_rows[:].bitcast(I32), 0)
+        nc.vector.memset(w_rows[:].bitcast(I32), 0)
         for w, scales in enumerate((w1_scales, w2_scales)):
             nc.scalar.dma_start(w_rows[0:16, w * H : (w + 1) * H].bitcast(I32), scales[0].bitcast(I32))
-        nc.scalar.dma_start(x_bytes[0:P:8, :].bitcast(I32), x_scales[0].bitcast(I32))
+        x_bytes = keep.tile([P, T], U8, name="x_bytes")
+        nc.vector.memset(x_bytes[:].bitcast(I32), 0)
 
         zero = keep.tile([P, 1], F32, name="zero")
         nc.vector.memset(zero[:], 0.0)
@@ -62,32 +73,33 @@ def tile_picked_dhlrelaypagez_none_p_kernel(tc, x_words, x_scales, w1_words, w1_
         w_raw = [keep.tile([P, H], U32, name="w_raw%d" % w) for w in range(2)]
         nc.sync.dma_start(w_raw[0][:].bitcast(I32), words_view(w1_words))
         n1_t = load_list("n1_t", n1)
-        x_win = shared.tile([P, T], U32, name="x_win", offset=0)
+        nc.sync.dma_start(x_bytes[0:P:8, :].bitcast(I32), x_scales[0].bitcast(I32))
+        x_win = shared.tile([P, T], U32, name="x_win", offset=AT_X_WORDS)
         nc.sync.dma_start(x_win[:].bitcast(I32), words_view(x_words))
-        for q in range(1, 4):
-            nc.sync.dma_start(w_rows[32 * q : 32 * q + 4, :].bitcast(I32), w_rows[4 * q : 4 * q + 4, :].bitcast(I32))
+        for q in range(1, QUADS):
+            nc.sync.dma_start(quad_rows(w_rows, q), w_rows[4 * q : 4 * q + 4, :].bitcast(I32))
         nc.sync.dma_start(w_raw[1][:].bitcast(I32), words_view(w2_words))
 
-        got_bytes = shared.tile([P, 2 * S], U8, name="got_bytes", offset=12288, align_bytes=64)
+        got_bytes = shared.tile([P, 2 * S], U8, name="got_bytes", offset=AT_GOT_BYTES, align_bytes=64)
         nc.vector.tensor_copy(got_bytes[:, 0:S], x_bytes[:].indirect(offs_t[:]))
         nc.vector.tensor_copy(got_bytes[:, S : 2 * S], x_bytes[:].indirect(hz_t[:]))
-        for q in range(4):
-            nc.sync.dma_start(x_plane[32 * q : 32 * q + 4, :].bitcast(I32), got_bytes[32 * q : 32 * q + 32 : 8, :].bitcast(I32))
-
+        for q in range(QUADS):
+            nc.sync.dma_start(quad_rows(x_plane, q), got_bytes[32 * q : 32 * q + 32 : 8, :].bitcast(I32))
 
         got_words = []
         for w, picks in enumerate((offs_t, hz_t)):
-            got = shared.tile([P, S], U32, name="got_words%d" % w, offset=24576 + 1024 * w, align_bytes=64)
+            got = shared.tile([P, S], U32, name="got_words%d" % w, offset=AT_PAGES + 2 * PAGE_BYTES + 4 * S * w, align_bytes=64)
             nc.vector.tensor_copy(got[:], x_win[:].indirect(picks[:]))
             got_words.append(got)
-        w_plane = [shared.tile([P, 2, P], U8, name="w_plane%d" % t, offset=256 * t, align_bytes=64) for t in range(PACK)]
+
+        w_plane = [shared.tile([P, 2, P], U8, name="w_plane%d" % t, offset=AT_X_WORDS + 2 * P * t, align_bytes=64) for t in range(PACK)]
         rows_by_tile = w_rows[:].rearrange("p (w m t) -> p w m t", w=2, t=PACK)
         for w in range(2):
             nc.vector.tensor_copy(w_plane[0][:, w, :], rows_by_tile[:, w, :, 0])
         for t in range(1, PACK):
             nc.vector.tensor_copy(w_plane[t][:], rows_by_tile[:, :, :, t])
 
-        w_dealt = [shared.tile([P, PACK, P], U32, name="w_dealt%d" % w, offset=16384 + 4096 * w, align_bytes=64) for w in range(2)]
+        w_dealt = [shared.tile([P, PACK, P], U32, name="w_dealt%d" % w, offset=AT_PAGES + PAGE_BYTES * w, align_bytes=64) for w in range(2)]
         raw_words = [raw[:].rearrange("p (m t) -> p m t", t=PACK) for raw in w_raw]
         nc.scalar.copy(w_dealt[0][:].rearrange("p t m -> p m t"), raw_words[0])
         nc.scalar.copy(w_dealt[1][:, 0, :], raw_words[1][:, :, 0])
@@ -96,20 +108,20 @@ def tile_picked_dhlrelaypagez_none_p_kernel(tc, x_words, x_scales, w1_words, w1_
         n2_t = load_list("n2_t", n2)
         n4_t = load_list("n4_t", n4)
         n3_t = load_list("n3_t", n3)
-        w3 = shared.tile([P, N], U32, name="w3", offset=12288, align_bytes=64)
+        w3 = shared.tile([P, N], U32, name="w3", offset=AT_GOT_BYTES, align_bytes=64)
         nc.sync.dma_start(w3[:].bitcast(I32), words_view(w3_words))
 
         w3_plane = keep.tile([P, N], U8, name="w3_plane", tag="rows", align_bytes=64)
         nc.vector.memset(w3_plane[:].bitcast(I32), 0)
-        for q in range(4):
-            nc.sync.dma_start(w3_plane[32 * q : 32 * q + 4, :].bitcast(I32), w3_scales[0].bitcast(I32)[4 * q : 4 * q + 4, :])
+        for q in range(QUADS):
+            nc.sync.dma_start(quad_rows(w3_plane, q), w3_scales[0].bitcast(I32)[4 * q : 4 * q + 4, :])
 
         y = []
         for t in range(PACK):
-            acc = psum.tile([P, S], F32, name="y_acc%d" % t, tag="bank%d" % t)
+            y_acc = psum.tile([P, S], F32, name="y_acc%d" % t, tag="bank%d" % t)
             for w in range(2):
                 nc.tensor.matmul_mx(
-                    out=acc[:],
+                    out=y_acc[:],
                     lhsT=w_dealt[w][:, t, :].bitcast(FP8X4),
                     lhsT_scale=w_plane[t][:, w, :],
                     rhs=got_words[w][:].bitcast(FP8X4),
@@ -118,52 +130,51 @@ def tile_picked_dhlrelaypagez_none_p_kernel(tc, x_words, x_scales, w1_words, w1_
                     stop=(w == 1),
                 )
             y_t = keep.tile([P, S], F32, name="y%d" % t)
-            nc.vector.tensor_copy(y_t[:], acc[:])
+            nc.vector.tensor_copy(y_t[:], y_acc[:])
             y.append(y_t)
 
         for m in range(1, N // P):
-            page = shared.tile([P, U], F32, name="page%d" % m, offset=16384 + 4096 * (m - 1))
+            page = shared.tile([P, U], F32, name="page%d" % m, offset=AT_PAGES + PAGE_BYTES * (m - 1))
             nc.vector.memset(page[:], 0.0)
             pages.append(page)
 
-        halves = [(0, HALF), (HALF, S)]
-        z = [keep.tile([P, HALF, PACK], BF16, name="z%d" % h, align_bytes=64) for h in range(2)]
+        z = [keep.tile([P, HALF, PACK], BF16, name="z%d" % c, align_bytes=64) for c in range(2)]
         ds = [keep.tile([P, WIN], F32, name="ds%d" % t) for t in range(PACK)]
 
         def send(t):
             nc.scalar.activation(ds[t][:].indirect(n1_t[:]), y[t][:], COPY)
 
         def compare(t, pieces):
-            fetched = keep.tile([P, S], F32, name="ds_got%d" % t)
+            ds_got = keep.tile([P, S], F32, name="ds_got%d" % t)
             larger = keep.tile([P, S], F32, name="larger%d" % t)
             for lo, hi in pieces:
-                nc.scalar.activation(fetched[:, lo:hi], ds[t][:].indirect(n2_t[:, lo // 16 : hi // 16]), COPY)
+                nc.scalar.activation(ds_got[:, lo:hi], ds[t][:].indirect(n2_t[:, lo // GROUP : hi // GROUP]), COPY)
             for lo, hi in pieces:
-                nc.vector.tensor_tensor(larger[:, lo:hi], fetched[:, lo:hi], y[t][:, lo:hi], ALU.max)
-            for h in range(2):
-                nc.vector.tensor_scalar(z[h][:, :, t], larger[:, h * HALF : (h + 1) * HALF], gain[:, t : t + 1], None, ALU.mult)
+                nc.vector.tensor_tensor(larger[:, lo:hi], ds_got[:, lo:hi], y[t][:, lo:hi], ALU.max)
+            for c, (lo, hi) in enumerate(HALVES):
+                nc.vector.tensor_scalar(z[c][:, :, t], larger[:, lo:hi], gain[:, t : t + 1], None, ALU.mult)
 
         send(0)
         send(1)
-        compare(0, [(0, S)])
+        compare(0, WHOLE)
         send(2)
-        compare(1, [(0, S)])
-        compare(2, [(0, S)])
+        compare(1, WHOLE)
+        compare(2, WHOLE)
         send(3)
-        compare(3, halves)
+        compare(3, HALVES)
 
         z_words = keep.tile([P, S], U32, name="z_words", align_bytes=64)
         z_plane = keep.tile([P, S], U8, name="z_plane", align_bytes=64)
-        for h, (lo, hi) in enumerate(halves):
-            nc.vector.quantize_mx(out=z_words[:, lo:hi].bitcast(FP8X4), scales=z_plane[:, lo:hi], in_=z[h][:].rearrange("p j t -> p (j t)"))
+        for c, (lo, hi) in enumerate(HALVES):
+            nc.vector.quantize_mx(out=z_words[:, lo:hi].bitcast(FP8X4), scales=z_plane[:, lo:hi], in_=z[c][:].rearrange("p j t -> p (j t)"))
 
         h_acc = []
         for m in range(N // P):
-            accs = []
-            for lo, hi in halves if m == 0 else [(0, S)]:
-                acc = psum.tile([P, hi - lo], F32, name="h_acc%d_%d" % (m, lo), tag="bank%d" % (m + 4 - 4 * (lo // HALF)))
+            parts = []
+            for lo, hi in HALVES if m == 0 else WHOLE:
+                part = psum.tile([P, hi - lo], F32, name="h_acc%d_%d" % (m, lo), tag="bank%d" % (m + PACK if lo == 0 else 0))
                 nc.tensor.matmul_mx(
-                    out=acc[:],
+                    out=part[:],
                     lhsT=w3[:, m * P : (m + 1) * P].bitcast(FP8X4),
                     lhsT_scale=w3_plane[:, m * P : (m + 1) * P],
                     rhs=z_words[:, lo:hi].bitcast(FP8X4),
@@ -171,20 +182,20 @@ def tile_picked_dhlrelaypagez_none_p_kernel(tc, x_words, x_scales, w1_words, w1_
                     start=True,
                     stop=True,
                 )
-                accs.append((acc, slice(lo, hi)))
-            h_acc.append(accs)
+                parts.append((part, slice(lo, hi)))
+            h_acc.append(parts)
 
         nw = []
 
         def fetch(m):
             positive = keep.tile([P, WIN], F32, name="positive%d" % m)
-            for acc, cols in h_acc[m]:
-                nc.vector.tensor_scalar(positive[:, cols], acc[:], 0.0, None, ALU.max)
-            fetched = keep.tile([P, S], F32, name="h_got%d" % m)
-            nc.scalar.activation(fetched[:], positive[:].indirect(n4_t[:]), COPY)
+            for part, cols in h_acc[m]:
+                nc.vector.tensor_scalar(positive[:, cols], part[:], 0.0, None, ALU.max)
+            h_got = keep.tile([P, S], F32, name="h_got%d" % m)
+            nc.scalar.activation(h_got[:], positive[:].indirect(n4_t[:]), COPY)
             nw_m = keep.tile([P, S], F32, name="nw%d" % m)
-            for acc, cols in h_acc[m]:
-                nc.vector.tensor_tensor(nw_m[:, cols], acc[:], fetched[:, cols], ALU.subtract)
+            for part, cols in h_acc[m]:
+                nc.vector.tensor_tensor(nw_m[:, cols], part[:], h_got[:, cols], ALU.subtract)
             nw.append(nw_m)
 
         def place(m):

from contextlib import ExitStack

import concourse.mybir as mybir

K, T, S, N, H, U = 512, 2048, 256, 512, 512, 1024
FLOPS = 2 * S * (2 * K * H + H * N)

F32 = mybir.dt.float32
BF16 = mybir.dt.bfloat16
I32 = mybir.dt.int32
U32 = mybir.dt.uint32
U16 = mybir.dt.uint16
U8 = mybir.dt.uint8
FP8X4 = mybir.dt.float8_e4m3fn_x4
ALU = mybir.AluOpType
COPY = mybir.ActivationFunctionType.Copy

P = 128
PACK = 4
QUADS = 4
GROUP = 16
HALF = S // 2
WHOLE = [(0, S)]
HALVES = [(0, HALF), (HALF, S)]
WIN = 2 * S

AT_X_WORDS = 0
AT_GOT_BYTES = 12288
AT_PAGES = 16384
PAGE_BYTES = 4 * U


def words_view(words):
    return words[0].rearrange("p n t -> p (n t)").bitcast(I32)


def tile_picked_dhlrelaypagez_none_p_kernel(tc, x_words, x_scales, w1_words, w1_scales, w2_words, w2_scales, gn, w3_words, w3_scales, offs, hz, n1, n2, n3, n4, out):
    nc = tc.nc
    with ExitStack() as ctx:
        lists = ctx.enter_context(tc.tile_pool(name="lists", bufs=1))
        keep = ctx.enter_context(tc.tile_pool(name="keep", bufs=1))
        shared = ctx.enter_context(tc.tile_pool(name="shared", bufs=1))
        psum = ctx.enter_context(tc.psum_pool(name="psum", bufs=1))

        def load_list(name, src):
            tile = lists.tile([P, S // GROUP], U16, name=name)
            nc.sync.dma_start(tile[:], src)
            return tile

        def quad_rows(plane, q):
            return plane[32 * q : 32 * q + 4, :].bitcast(I32)

        offs_t = load_list("offs_t", offs)
        hz_t = load_list("hz_t", hz)

        w_rows = keep.tile([P, 2 * H], U8, name="w_rows", tag="rows", align_bytes=64)
        nc.vector.memset(w_rows[:].bitcast(I32), 0)
        for w, scales in enumerate((w1_scales, w2_scales)):
            nc.scalar.dma_start(w_rows[0:16, w * H : (w + 1) * H].bitcast(I32), scales[0].bitcast(I32))
        x_bytes = keep.tile([P, T], U8, name="x_bytes")
        nc.vector.memset(x_bytes[:].bitcast(I32), 0)

        zero = keep.tile([P, 1], F32, name="zero")
        nc.vector.memset(zero[:], 0.0)
        pages = [keep.tile([P, U], F32, name="page0")]
        nc.scalar.activation(pages[0][:], zero[:].to_broadcast([P, U]), COPY)

        gain = keep.tile([P, PACK], F32, name="gain")
        nc.gpsimd.dma_start(gain[:], gn.rearrange("(p t) o -> p (t o)", t=PACK))
        x_plane = keep.tile([P, 2 * S], U8, name="x_plane", align_bytes=64)
        nc.vector.memset(x_plane[:].bitcast(I32), 0)

        w_raw = [keep.tile([P, H], U32, name="w_raw%d" % w) for w in range(2)]
        nc.sync.dma_start(w_raw[0][:].bitcast(I32), words_view(w1_words))
        n1_t = load_list("n1_t", n1)
        nc.sync.dma_start(x_bytes[0:P:8, :].bitcast(I32), x_scales[0].bitcast(I32))
        x_win = shared.tile([P, T], U32, name="x_win", offset=AT_X_WORDS)
        nc.sync.dma_start(x_win[:].bitcast(I32), words_view(x_words))
        for q in range(1, QUADS):
            nc.sync.dma_start(quad_rows(w_rows, q), w_rows[4 * q : 4 * q + 4, :].bitcast(I32))
        nc.sync.dma_start(w_raw[1][:].bitcast(I32), words_view(w2_words))

        got_bytes = shared.tile([P, 2 * S], U8, name="got_bytes", offset=AT_GOT_BYTES, align_bytes=64)
        nc.vector.tensor_copy(got_bytes[:, 0:S], x_bytes[:].indirect(offs_t[:]))
        nc.vector.tensor_copy(got_bytes[:, S : 2 * S], x_bytes[:].indirect(hz_t[:]))
        for q in range(QUADS):
            nc.sync.dma_start(quad_rows(x_plane, q), got_bytes[32 * q : 32 * q + 32 : 8, :].bitcast(I32))

        got_words = []
        for w, picks in enumerate((offs_t, hz_t)):
            got = shared.tile([P, S], U32, name="got_words%d" % w, offset=AT_PAGES + 2 * PAGE_BYTES + 4 * S * w, align_bytes=64)
            nc.vector.tensor_copy(got[:], x_win[:].indirect(picks[:]))
            got_words.append(got)

        w_plane = [shared.tile([P, 2, P], U8, name="w_plane%d" % t, offset=AT_X_WORDS + 2 * P * t, align_bytes=64) for t in range(PACK)]
        rows_by_tile = w_rows[:].rearrange("p (w m t) -> p w m t", w=2, t=PACK)
        for w in range(2):
            nc.vector.tensor_copy(w_plane[0][:, w, :], rows_by_tile[:, w, :, 0])
        for t in range(1, PACK):
            nc.vector.tensor_copy(w_plane[t][:], rows_by_tile[:, :, :, t])

        w_dealt = [shared.tile([P, PACK, P], U32, name="w_dealt%d" % w, offset=AT_PAGES + PAGE_BYTES * w, align_bytes=64) for w in range(2)]
        raw_words = [raw[:].rearrange("p (m t) -> p m t", t=PACK) for raw in w_raw]
        nc.scalar.copy(w_dealt[0][:].rearrange("p t m -> p m t"), raw_words[0])
        nc.scalar.copy(w_dealt[1][:, 0, :], raw_words[1][:, :, 0])
        nc.scalar.copy(w_dealt[1][:, 1:PACK, :].rearrange("p t m -> p m t"), raw_words[1][:, :, 1:PACK])

        n2_t = load_list("n2_t", n2)
        n4_t = load_list("n4_t", n4)
        n3_t = load_list("n3_t", n3)
        w3 = shared.tile([P, N], U32, name="w3", offset=AT_GOT_BYTES, align_bytes=64)
        nc.sync.dma_start(w3[:].bitcast(I32), words_view(w3_words))

        w3_plane = keep.tile([P, N], U8, name="w3_plane", tag="rows", align_bytes=64)
        nc.vector.memset(w3_plane[:].bitcast(I32), 0)
        for q in range(QUADS):
            nc.sync.dma_start(quad_rows(w3_plane, q), w3_scales[0].bitcast(I32)[4 * q : 4 * q + 4, :])

        y = []
        for t in range(PACK):
            y_acc = psum.tile([P, S], F32, name="y_acc%d" % t, tag="bank%d" % t)
            for w in range(2):
                nc.tensor.matmul_mx(
                    out=y_acc[:],
                    lhsT=w_dealt[w][:, t, :].bitcast(FP8X4),
                    lhsT_scale=w_plane[t][:, w, :],
                    rhs=got_words[w][:].bitcast(FP8X4),
                    rhs_scale=x_plane[:, w * S : (w + 1) * S],
                    start=(w == 0),
                    stop=(w == 1),
                )
            y_t = keep.tile([P, S], F32, name="y%d" % t)
            nc.vector.tensor_copy(y_t[:], y_acc[:])
            y.append(y_t)

        for m in range(1, N // P):
            page = shared.tile([P, U], F32, name="page%d" % m, offset=AT_PAGES + PAGE_BYTES * (m - 1))
            nc.vector.memset(page[:], 0.0)
            pages.append(page)

        z = [keep.tile([P, HALF, PACK], BF16, name="z%d" % c, align_bytes=64) for c in range(2)]
        ds = [keep.tile([P, WIN], F32, name="ds%d" % t) for t in range(PACK)]

        def send(t):
            nc.scalar.activation(ds[t][:].indirect(n1_t[:]), y[t][:], COPY)

        def compare(t, pieces):
            ds_got = keep.tile([P, S], F32, name="ds_got%d" % t)
            larger = keep.tile([P, S], F32, name="larger%d" % t)
            for lo, hi in pieces:
                nc.scalar.activation(ds_got[:, lo:hi], ds[t][:].indirect(n2_t[:, lo // GROUP : hi // GROUP]), COPY)
            for lo, hi in pieces:
                nc.vector.tensor_tensor(larger[:, lo:hi], ds_got[:, lo:hi], y[t][:, lo:hi], ALU.max)
            for c, (lo, hi) in enumerate(HALVES):
                nc.vector.tensor_scalar(z[c][:, :, t], larger[:, lo:hi], gain[:, t : t + 1], None, ALU.mult)

        send(0)
        send(1)
        compare(0, WHOLE)
        send(2)
        compare(1, WHOLE)
        compare(2, WHOLE)
        send(3)
        compare(3, HALVES)

        z_words = keep.tile([P, S], U32, name="z_words", align_bytes=64)
        z_plane = keep.tile([P, S], U8, name="z_plane", align_bytes=64)
        for c, (lo, hi) in enumerate(HALVES):
            nc.vector.quantize_mx(out=z_words[:, lo:hi].bitcast(FP8X4), scales=z_plane[:, lo:hi], in_=z[c][:].rearrange("p j t -> p (j t)"))

        h_acc = []
        for m in range(N // P):
            parts = []
            for lo, hi in HALVES if m == 0 else WHOLE:
                part = psum.tile([P, hi - lo], F32, name="h_acc%d_%d" % (m, lo), tag="bank%d" % (m + PACK if lo == 0 else 0))
                nc.tensor.matmul_mx(
                    out=part[:],
                    lhsT=w3[:, m * P : (m + 1) * P].bitcast(FP8X4),
                    lhsT_scale=w3_plane[:, m * P : (m + 1) * P],
                    rhs=z_words[:, lo:hi].bitcast(FP8X4),
                    rhs_scale=z_plane[:, lo:hi],
                    start=True,
                    stop=True,
                )
                parts.append((part, slice(lo, hi)))
            h_acc.append(parts)

        nw = []

        def fetch(m):
            positive = keep.tile([P, WIN], F32, name="positive%d" % m)
            for part, cols in h_acc[m]:
                nc.vector.tensor_scalar(positive[:, cols], part[:], 0.0, None, ALU.max)
            h_got = keep.tile([P, S], F32, name="h_got%d" % m)
            nc.scalar.activation(h_got[:], positive[:].indirect(n4_t[:]), COPY)
            nw_m = keep.tile([P, S], F32, name="nw%d" % m)
            for part, cols in h_acc[m]:
                nc.vector.tensor_tensor(nw_m[:, cols], part[:], h_got[:, cols], ALU.subtract)
            nw.append(nw_m)

        def place(m):
            nc.scalar.activation(pages[m][:].indirect(n3_t[:]), nw[m][:], COPY)
            nc.sync.dma_start(out[m * P : (m + 1) * P, :], pages[m][:])

        fetch(0)
        for m in range(1, N // P):
            fetch(m)
            place(m - 1)
        place(N // P - 1)
